import numpy as np, ml_dtypes
CORES = [3,0,2,1,6,7,4,5]
N = 8
COUNTS = [[1,2,18,3,1,2,6,3],[3,1,6,6,3,1,2,6],[6,3,3,2,6,3,1,2],[2,6,9,1,2,6,3,1],[1,2,18,3,1,2,6,3],[3,1,6,6,3,1,2,6],[6,3,3,2,6,3,1,2],[2,6,9,1,2,6,3,1]]
XW, YW = 36, 72
def setup_inputs(rng):
    return {"x": rng.standard_normal((N, 128, XW), dtype=np.float32).astype(ml_dtypes.bfloat16)}
def reference(x):
    y = np.full((N, 128, YW), np.nan, x.dtype)
    fill = [0] * N
    for s in range(N):
        o = 0
        for d in range(N):
            c = COUNTS[s][d]
            y[d][:, fill[d]:fill[d] + c] = x[s][:, o:o + c]
            o += c; fill[d] += c
    return {"y": y}

from concourse.bass import DstId, RemoteDMATransfer

SCRATCH = {
    "xs": ("sbuf", [128, 36], "bfloat16"),
    "land": ("sbuf", [128, 72], "bfloat16"),
}
SEMAPHORES = ["loaded", "read", "arrived", "stored"]


def rank_program(g, core, T, topo):
    rank = T.rank_of(core)
    if rank is None:
        return
    counts = T.tables["COUNTS"]
    n = len(counts)

    def src_col(s, d):
        return sum(counts[s][:d])

    def dst_col(s, d):
        return sum(counts[k][d] for k in range(s))

    def calls_of(s):
        groups = {}
        for d in range(n):
            if d != s and counts[s][d] > 0:
                groups.setdefault(counts[s][d], []).append(d)
        calls = []
        for width in sorted(groups):
            dsts = groups[width]
            engines = 16
            while engines * len(dsts) > 16:
                engines //= 2
            calls.append((width, engines, dsts))
        return calls

    used = sum(counts[rank])
    total = sum(counts[s][rank] for s in range(n))

    g.dma_start(T.xs[:, 0:used], T.x[:, 0:used]).then_inc(T.sem.loaded, 16)
    loaded = 16
    g.wait_ge(T.sem.loaded, loaded)

    sent = 0
    for width, engines, dsts in calls_of(rank):
        transfers = []
        for j, d in enumerate(dsts):
            rid, pid, sengine = topo.addr(T.cores[d])
            a, b = src_col(rank, d), dst_col(rank, d)
            transfers.append(RemoteDMATransfer(
                dst_ids=[DstId(rid=rid, pnc=pid)],
                dma_engine_mask=((1 << engines) - 1) << (j * engines),
                remote_sem=T.sem.arrived,
                src=T.xs[:, a:a + width],
                dst=T.land[:, b:b + width],
            ))
            sent += engines
        g.remote_dma_fused(transfers, local_sem=T.sem.read)

    own = counts[rank][rank]
    if own > 0:
        a, b = src_col(rank, rank), dst_col(rank, rank)
        g.dma_start(T.land[:, b:b + own], T.xs[:, a:a + own]).then_inc(T.sem.loaded, 16)
        loaded += 16
        g.wait_ge(T.sem.loaded, loaded)

    expected = 0
    for s in range(n):
        for width, engines, dsts in calls_of(s):
            if rank in dsts:
                expected += engines
    if expected > 0:
        g.wait_ge(T.sem.arrived, expected)
    g.dma_start(T.y[:, 0:total], T.land[:, 0:total]).then_inc(T.sem.stored, 16)
    g.wait_ge(T.sem.stored, 16)
    if sent > 0:
        g.wait_ge(T.sem.read, sent)
